import numpy as np
import ml_dtypes

BF16 = ml_dtypes.bfloat16


def bf(x):
    return np.asarray(x, np.float32).astype(BF16)


def f32(x):
    return np.asarray(x, np.float32)


def f64(x):
    return np.asarray(x).astype(np.float64)


def striped(idx):
    return np.tile(idx.reshape(-1, 16).T, (8, 1))


S, K, M, N, E, Q = 512, 128, 256, 384, 2, 192


def setup_inputs():
    return {"base": bf(np.random.standard_normal((M, S))), "x": bf(np.random.standard_normal((K, N))), "w": bf(np.random.standard_normal((E, K, M)) / np.sqrt(K)), "b": f32(0.5 * np.random.standard_normal((M, 1))), "offs": striped(np.random.permutation(S)[:N])}


def reference(base, x, w, b, offs):
    idx = offs[:16].T.reshape(-1)
    z = f64(base).copy()
    for e in range(E):
        z[:, idx[e * Q : (e + 1) * Q]] = f64(w)[e].T @ f64(x)[:, e * Q : (e + 1) * Q]
    return np.maximum(z + f64(b), 0.0)

@@ -1,0 +1,62 @@
+import concourse.mybir as mybir
+from concourse.masks import make_identity
+
+BF16, F32, U16 = mybir.dt.bfloat16, mybir.dt.float32, mybir.dt.uint16
+RELU = mybir.ActivationFunctionType.Relu
+ADD, MAX = mybir.AluOpType.add, mybir.AluOpType.max
+
+P = 128
+TOKENS = 512
+FEATURES = 256
+BLOCKS = FEATURES // P
+EXPERTS = 2
+PIECE = 192
+PIECE_COLS = PIECE // 16
+
+FLOPS = 2 * P * FEATURES * EXPERTS * PIECE
+
+
+def tile_scatter_matmul_kernel(tc, base, x, w, b, offs, out):
+    nc = tc.nc
+    with (
+        tc.tile_pool(name="held", bufs=1) as held,
+        tc.psum_pool(name="windows", bufs=1) as windows,
+    ):
+        offsets = held.tile([P, EXPERTS * PIECE_COLS], U16, name="offsets")
+        nc.sync.dma_start(offsets[:], offs)
+
+        base_sb = [held.tile([P, TOKENS], BF16, name=f"base{a}") for a in range(BLOCKS)]
+        nc.sync.dma_start(base_sb[0][:], base[0:P, :])
+        nc.scalar.dma_start(base_sb[1][:], base[P : 2 * P, :])
+
+        x_sb = held.tile([P, EXPERTS * PIECE], BF16, name="x_sb")
+        nc.sync.dma_start(x_sb[:], x)
+        w_sb = held.tile([P, EXPERTS, FEATURES], BF16, name="w_sb")
+        nc.scalar.dma_start(w_sb[:], w.rearrange("e k m -> k e m"))
+
+        bias = held.tile([P, BLOCKS], F32, name="bias")
+        with nc.allow_non_contiguous_dma(reason="256 single floats, one to a partition"):
+            nc.scalar.dma_start(bias[:], b.rearrange("(a p) o -> p (a o)", p=P))
+
+        ident = held.tile([P, P], BF16, name="ident")
+        make_identity(nc, ident[:])
+
+        window = [windows.tile([P, TOKENS], F32, name=f"window{a}") for a in range(BLOCKS)]
+        for a in range(BLOCKS):
+            nc.tensor.matmul(window[a][:], ident[:], base_sb[a][:], start=True, stop=True)
+
+        for a in range(BLOCKS):
+            for e in range(EXPERTS):
+                nc.tensor.matmul(
+                    window[a][:].indirect(offsets[:, e * PIECE_COLS : (e + 1) * PIECE_COLS]),
+                    w_sb[:, e, a * P : (a + 1) * P],
+                    x_sb[:, e * PIECE : (e + 1) * PIECE],
+                    start=True,
+                    stop=True,
+                )
+
+        result = [held.tile([P, TOKENS], F32, name=f"result{a}") for a in range(BLOCKS)]
+        nc.scalar.activation(result[0][:], window[0][:], RELU, bias=bias[:, 0:1])
+        nc.sync.dma_start(out[0:P, :], result[0][:])
+        nc.vector.tensor_scalar(result[1][:], window[1][:], bias[:, 1:2], 0.0, op0=ADD, op1=MAX)
+        nc.scalar.dma_start(out[P : 2 * P, :], result[1][:])

@@ -13,6 +13,8 @@ EXPERTS = 2
 PIECE = 192
 PIECE_COLS = PIECE // 16
 
+WARMUP = 4
+
 FLOPS = 2 * P * FEATURES * EXPERTS * PIECE
 
 
@@ -22,6 +24,12 @@ def tile_scatter_matmul_kernel(tc, base, x, w, b, offs, out):
         tc.tile_pool(name="held", bufs=1) as held,
         tc.psum_pool(name="windows", bufs=1) as windows,
     ):
+        zeros = held.tile([P, TOKENS], BF16, name="zeros")
+        nc.vector.memset(zeros[:], 0.0)
+        unread = windows.tile([P, TOKENS], F32, name="unread")
+        for i in range(WARMUP):
+            nc.tensor.matmul(unread[:], zeros[:, 0:P], zeros[:], start=True, stop=True)
+
         offsets = held.tile([P, EXPERTS * PIECE_COLS], U16, name="offsets")
         nc.sync.dma_start(offsets[:], offs)
 

@@ -24,15 +24,21 @@ def tile_scatter_matmul_kernel(tc, base, x, w, b, offs, out):
         tc.tile_pool(name="held", bufs=1) as held,
         tc.psum_pool(name="windows", bufs=1) as windows,
     ):
-        zeros = held.tile([P, TOKENS], BF16, name="zeros")
+        zeros = held.tile([P, P], BF16, name="zeros")
         nc.vector.memset(zeros[:], 0.0)
         unread = windows.tile([P, TOKENS], F32, name="unread")
         for i in range(WARMUP):
-            nc.tensor.matmul(unread[:], zeros[:, 0:P], zeros[:], start=True, stop=True)
+            nc.tensor.matmul(
+                unread[:].rearrange("p (r c) -> p r c", c=P),
+                zeros[:],
+                zeros[:].unsqueeze(1).to_broadcast([P, TOKENS // P, P]),
+                start=True,
+                stop=True,
+            )
 
-        offsets = held.tile([P, EXPERTS * PIECE_COLS], U16, name="offsets")
-        nc.sync.dma_start(offsets[:], offs)
-
+        bias = held.tile([P, BLOCKS], F32, name="bias")
+        with nc.allow_non_contiguous_dma(reason="256 single floats, one to a partition"):
+            nc.scalar.dma_start(bias[:], b.rearrange("(a p) o -> p (a o)", p=P))
         base_sb = [held.tile([P, TOKENS], BF16, name=f"base{a}") for a in range(BLOCKS)]
         nc.sync.dma_start(base_sb[0][:], base[0:P, :])
         nc.scalar.dma_start(base_sb[1][:], base[P : 2 * P, :])
@@ -42,9 +48,8 @@ def tile_scatter_matmul_kernel(tc, base, x, w, b, offs, out):
         w_sb = held.tile([P, EXPERTS, FEATURES], BF16, name="w_sb")
         nc.scalar.dma_start(w_sb[:], w.rearrange("e k m -> k e m"))
 
-        bias = held.tile([P, BLOCKS], F32, name="bias")
-        with nc.allow_non_contiguous_dma(reason="256 single floats, one to a partition"):
-            nc.scalar.dma_start(bias[:], b.rearrange("(a p) o -> p (a o)", p=P))
+        offsets = held.tile([P, EXPERTS * PIECE_COLS], U16, name="offsets")
+        nc.sync.dma_start(offsets[:], offs)
 
         ident = held.tile([P, P], BF16, name="ident")
         make_identity(nc, ident[:])
@@ -64,7 +69,7 @@ def tile_scatter_matmul_kernel(tc, base, x, w, b, offs, out):
                 )
 
         result = [held.tile([P, TOKENS], F32, name=f"result{a}") for a in range(BLOCKS)]
-        nc.scalar.activation(result[0][:], window[0][:], RELU, bias=bias[:, 0:1])
+        nc.vector.tensor_scalar(result[0][:], window[0][:], bias[:, 0:1], 0.0, op0=ADD, op1=MAX)
         nc.sync.dma_start(out[0:P, :], result[0][:])
-        nc.vector.tensor_scalar(result[1][:], window[1][:], bias[:, 1:2], 0.0, op0=ADD, op1=MAX)
+        nc.scalar.activation(result[1][:], window[1][:], RELU, bias=bias[:, 1:2])
         nc.scalar.dma_start(out[P : 2 * P, :], result[1][:])

@@ -36,9 +36,6 @@ def tile_scatter_matmul_kernel(tc, base, x, w, b, offs, out):
                 stop=True,
             )
 
-        bias = held.tile([P, BLOCKS], F32, name="bias")
-        with nc.allow_non_contiguous_dma(reason="256 single floats, one to a partition"):
-            nc.scalar.dma_start(bias[:], b.rearrange("(a p) o -> p (a o)", p=P))
         base_sb = [held.tile([P, TOKENS], BF16, name=f"base{a}") for a in range(BLOCKS)]
         nc.sync.dma_start(base_sb[0][:], base[0:P, :])
         nc.scalar.dma_start(base_sb[1][:], base[P : 2 * P, :])
@@ -47,6 +44,13 @@ def tile_scatter_matmul_kernel(tc, base, x, w, b, offs, out):
         nc.sync.dma_start(x_sb[:], x)
         w_sb = held.tile([P, EXPERTS, FEATURES], BF16, name="w_sb")
         nc.scalar.dma_start(w_sb[:], w.rearrange("e k m -> k e m"))
+
+        bias = held.tile([P, BLOCKS], F32, name="bias")
+        with nc.allow_non_contiguous_dma(reason="256 single floats, one to a partition"):
+            nc.scalar.dma_start(bias[:], b.rearrange("(a p) o -> p (a o)", p=P))
+
+        early = held.tile([P, 1], F32, name="early")
+        nc.scalar.activation(early[:], zeros[:, 0:1], RELU)
 
         offsets = held.tile([P, EXPERTS * PIECE_COLS], U16, name="offsets")
         nc.sync.dma_start(offsets[:], offs)

@@ -7,6 +7,7 @@ ADD, MAX = mybir.AluOpType.add, mybir.AluOpType.max
 
 P = 128
 TOKENS = 512
+HALF = TOKENS // 2
 FEATURES = 256
 BLOCKS = FEATURES // P
 EXPERTS = 2
@@ -73,7 +74,12 @@ def tile_scatter_matmul_kernel(tc, base, x, w, b, offs, out):
                 )
 
         result = [held.tile([P, TOKENS], F32, name=f"result{a}") for a in range(BLOCKS)]
-        nc.vector.tensor_scalar(result[0][:], window[0][:], bias[:, 0:1], 0.0, op0=ADD, op1=MAX)
-        nc.sync.dma_start(out[0:P, :], result[0][:])
-        nc.scalar.activation(result[1][:], window[1][:], RELU, bias=bias[:, 1:2])
-        nc.scalar.dma_start(out[P : 2 * P, :], result[1][:])
+        for h in range(2):
+            cols = slice(h * HALF, (h + 1) * HALF)
+            nc.vector.tensor_scalar(result[0][:, cols], window[0][:, cols], bias[:, 0:1], 0.0, op0=ADD, op1=MAX)
+            nc.sync.dma_start(out[0:P, cols], result[0][:, cols])
+        for h in range(2):
+            cols = slice(h * HALF, (h + 1) * HALF)
+            nc.scalar.activation(result[1][:, cols], window[1][:, cols], RELU, bias=bias[:, 1:2])
+        nc.sync.dma_start(out[P : 2 * P, 0:HALF], result[1][:, 0:HALF])
+        nc.scalar.dma_start(out[P : 2 * P, HALF:TOKENS], result[1][:, HALF:TOKENS])

@@ -26,7 +26,7 @@ def tile_scatter_matmul_kernel(tc, base, x, w, b, offs, out):
         tc.psum_pool(name="windows", bufs=1) as windows,
     ):
         zeros = held.tile([P, P], BF16, name="zeros")
-        nc.vector.memset(zeros[:], 0.0)
+        nc.gpsimd.memset(zeros[:], 0.0)
         unread = windows.tile([P, TOKENS], F32, name="unread")
         for i in range(WARMUP):
             nc.tensor.matmul(

@@ -14,7 +14,7 @@ EXPERTS = 2
 PIECE = 192
 PIECE_COLS = PIECE // 16
 
-WARMUP = 4
+WARMUP = 3
 
 FLOPS = 2 * P * FEATURES * EXPERTS * PIECE
 

@@ -41,10 +41,13 @@ def tile_scatter_matmul_kernel(tc, base, x, w, b, offs, out):
         nc.sync.dma_start(base_sb[0][:], base[0:P, :])
         nc.scalar.dma_start(base_sb[1][:], base[P : 2 * P, :])
 
+        offsets = held.tile([P, EXPERTS * PIECE_COLS], U16, name="offsets")
+        nc.sync.dma_start(offsets[:], offs)
+
         x_sb = held.tile([P, EXPERTS * PIECE], BF16, name="x_sb")
-        nc.sync.dma_start(x_sb[:], x)
+        nc.scalar.dma_start(x_sb[:], x)
         w_sb = held.tile([P, EXPERTS, FEATURES], BF16, name="w_sb")
-        nc.scalar.dma_start(w_sb[:], w.rearrange("e k m -> k e m"))
+        nc.sync.dma_start(w_sb[:], w.rearrange("e k m -> k e m"))
 
         bias = held.tile([P, BLOCKS], F32, name="bias")
         with nc.allow_non_contiguous_dma(reason="256 single floats, one to a partition"):
@@ -52,9 +55,6 @@ def tile_scatter_matmul_kernel(tc, base, x, w, b, offs, out):
 
         early = held.tile([P, 1], F32, name="early")
         nc.scalar.activation(early[:], zeros[:, 0:1], RELU)
-
-        offsets = held.tile([P, EXPERTS * PIECE_COLS], U16, name="offsets")
-        nc.sync.dma_start(offsets[:], offs)
 
         ident = held.tile([P, P], BF16, name="ident")
         make_identity(nc, ident[:])

import concourse.mybir as mybir
from concourse.masks import make_identity

BF16, F32, U16 = mybir.dt.bfloat16, mybir.dt.float32, mybir.dt.uint16
RELU = mybir.ActivationFunctionType.Relu
ADD, MAX = mybir.AluOpType.add, mybir.AluOpType.max

P = 128
TOKENS = 512
HALF = TOKENS // 2
FEATURES = 256
BLOCKS = FEATURES // P
EXPERTS = 2
PIECE = 192
PIECE_COLS = PIECE // 16

WARMUP = 3

FLOPS = 2 * P * FEATURES * EXPERTS * PIECE


def tile_scatter_matmul_kernel(tc, base, x, w, b, offs, out):
    nc = tc.nc
    with (
        tc.tile_pool(name="held", bufs=1) as held,
        tc.psum_pool(name="windows", bufs=1) as windows,
    ):
        zeros = held.tile([P, P], BF16, name="zeros")
        nc.gpsimd.memset(zeros[:], 0.0)
        unread = windows.tile([P, TOKENS], F32, name="unread")
        for i in range(WARMUP):
            nc.tensor.matmul(
                unread[:].rearrange("p (r c) -> p r c", c=P),
                zeros[:],
                zeros[:].unsqueeze(1).to_broadcast([P, TOKENS // P, P]),
                start=True,
                stop=True,
            )

        base_sb = [held.tile([P, TOKENS], BF16, name=f"base{a}") for a in range(BLOCKS)]
        nc.sync.dma_start(base_sb[0][:], base[0:P, :])
        nc.scalar.dma_start(base_sb[1][:], base[P : 2 * P, :])

        offsets = held.tile([P, EXPERTS * PIECE_COLS], U16, name="offsets")
        nc.sync.dma_start(offsets[:], offs)

        x_sb = held.tile([P, EXPERTS * PIECE], BF16, name="x_sb")
        nc.scalar.dma_start(x_sb[:], x)
        w_sb = held.tile([P, EXPERTS, FEATURES], BF16, name="w_sb")
        nc.sync.dma_start(w_sb[:], w.rearrange("e k m -> k e m"))

        bias = held.tile([P, BLOCKS], F32, name="bias")
        with nc.allow_non_contiguous_dma(reason="256 single floats, one to a partition"):
            nc.scalar.dma_start(bias[:], b.rearrange("(a p) o -> p (a o)", p=P))

        early = held.tile([P, 1], F32, name="early")
        nc.scalar.activation(early[:], zeros[:, 0:1], RELU)

        ident = held.tile([P, P], BF16, name="ident")
        make_identity(nc, ident[:])

        window = [windows.tile([P, TOKENS], F32, name=f"window{a}") for a in range(BLOCKS)]
        for a in range(BLOCKS):
            nc.tensor.matmul(window[a][:], ident[:], base_sb[a][:], start=True, stop=True)

        for a in range(BLOCKS):
            for e in range(EXPERTS):
                nc.tensor.matmul(
                    window[a][:].indirect(offsets[:, e * PIECE_COLS : (e + 1) * PIECE_COLS]),
                    w_sb[:, e, a * P : (a + 1) * P],
                    x_sb[:, e * PIECE : (e + 1) * PIECE],
                    start=True,
                    stop=True,
                )

        result = [held.tile([P, TOKENS], F32, name=f"result{a}") for a in range(BLOCKS)]
        for h in range(2):
            cols = slice(h * HALF, (h + 1) * HALF)
            nc.vector.tensor_scalar(result[0][:, cols], window[0][:, cols], bias[:, 0:1], 0.0, op0=ADD, op1=MAX)
            nc.sync.dma_start(out[0:P, cols], result[0][:, cols])
        for h in range(2):
            cols = slice(h * HALF, (h + 1) * HALF)
            nc.scalar.activation(result[1][:, cols], window[1][:, cols], RELU, bias=bias[:, 1:2])
        nc.sync.dma_start(out[P : 2 * P, 0:HALF], result[1][:, 0:HALF])
        nc.scalar.dma_start(out[P : 2 * P, HALF:TOKENS], result[1][:, HALF:TOKENS])
